import numpy as np
import ml_dtypes


def mxq(x, axis, fmt="e4m3"):
    dtype, down = {"e4m3": (ml_dtypes.float8_e4m3fn, 7), "e5m2": (ml_dtypes.float8_e5m2, 14)}[fmt]
    v = np.moveaxis(np.asarray(x, np.float32).astype(ml_dtypes.bfloat16).astype(np.float64), axis, -1)
    blocks = v.reshape(v.shape[:-1] + (-1, 32))
    amax = np.abs(blocks).max(-1, keepdims=True)
    byte = np.maximum(np.where(amax > 0, np.frexp(amax)[1] - 1 + 127, 0) - down, 1)
    scale = np.exp2(byte - 127.0)
    codes = (blocks / scale).astype(np.float32).astype(dtype).astype(np.float64)
    return np.moveaxis((codes * scale).reshape(v.shape), -1, axis)


WIDE = False


def mx_kscale(k):
    if not WIDE:
        return np.ones(k)
    levels = np.array([10, -10, 5, -5, 0])
    if k % 512:
        return np.exp2(np.random.permutation(np.resize(levels, k // 32))).repeat(32)
    a = np.empty((k // 512, 16))
    for p in range(k // 512):
        a[p, :8] = np.random.permutation(np.resize(levels, 8))
        for g in range(8):
            far = levels[np.abs(levels - a[p, g]) >= 10]
            a[p, g + 8] = far[np.random.randint(len(far))]
    return np.exp2(a.ravel()).repeat(32)


def f64(x):
    return np.asarray(x).astype(np.float64)


def striped(idx):
    return np.tile(idx.reshape(-1, 16).T, (8, 1)).astype(np.uint16)


def unstriped(offs):
    return offs[:16].T.reshape(-1).astype(np.int64)


def striped8(idx):
    return np.concatenate([x.reshape(-1, 16).T for x in idx]).astype(np.uint16)


def runs(offs, k):
    lists = np.stack([offs[16 * r : 16 * r + 16].T.reshape(-1) for r in range(8)]).astype(np.int64)
    return lists[np.arange(k) % 512 // 64]


def pack_weight(w):
    k, n = w.shape
    w = f64(np.asarray(w, np.float32).astype(ml_dtypes.bfloat16)).reshape(k // 32, 32, n)
    amax = np.abs(w).max(1)
    byte = np.clip(np.where(amax > 0, np.frexp(amax)[1] - 1 + 127 - 7, 1), 1, 254)
    scaled = (w * np.exp2(127.0 - byte)[:, None, :]).reshape(k, n).astype(np.float32)
    words = np.ascontiguousarray(scaled.reshape(k // 512, 128, 4, n).transpose(0, 1, 3, 2)).astype(ml_dtypes.float8_e4m3fn).view(np.uint8)
    return words, np.ascontiguousarray(byte.astype(np.uint8).reshape(k // 512, 16, n))


def unpack_weight(words, scales):
    g, p, n, _ = words.shape
    vals = np.ascontiguousarray(words).view(ml_dtypes.float8_e4m3fn).astype(np.float64) * np.repeat(np.exp2(scales.astype(np.float64) - 127.0), 8, axis=1)[..., None]
    return vals.transpose(0, 1, 3, 2).reshape(g * 512, n)


def sigmoid(v):
    return 1.0 / (1.0 + np.exp(-np.maximum(v, -700.0)))


K, T, S, N, G, H = 512, 2048, 512, 512, 2048, 512


def setup_inputs():
    n = np.random.standard_normal
    s = mx_kscale(K)[:, None]
    u = mx_kscale(S)
    packed_xT = pack_weight(n((K, T)) * s)
    packed_dT = pack_weight(n((K, G)) / s)
    return {
        "x_words": packed_xT[0],
        "x_scales": packed_xT[1],
        "d_words": packed_dT[0],
        "d_scales": packed_dT[1],
        "gn": (np.random.uniform(0.5, 1.5, (H, 1)) * u[:, None]).astype(np.float32),
        "w1": (n((H, N)) / np.sqrt(2 * H) / u[:, None]).astype(np.float32),
        "w2": (n((K, N)) / np.sqrt(2 * K) / s).astype(np.float32),
        "offs": striped(np.random.permutation(T)[:S]),
        "k1": striped8(np.random.randint(0, G, (8, H))),
        "n1": striped(np.random.permutation(S)),
        "n2": striped(np.random.permutation(S)),
        "two": striped(np.random.permutation(T)[:S]),
        "n3": striped8(np.stack([np.random.permutation(S) for _ in range(8)])),
        "n4": striped8(np.stack([np.random.permutation(S) for _ in range(8)])),
    }


def reference(x_words, x_scales, d_words, d_scales, gn, w1, w2, offs, k1, n1, n2, two, n3, n4):
    d_k1 = unpack_weight(d_words, d_scales)[np.arange(K)[:, None], runs(k1, K)]
    xq = unpack_weight(x_words, x_scales)[:, unstriped(offs)]
    s = 0.0625 * (d_k1.T @ xq)
    z = f64(gn) * (s - (np.minimum(s[:, unstriped(n1)], s[:, unstriped(n2)])))
    x_two = unpack_weight(x_words, x_scales)[:, unstriped(two)]
    h = mxq(f64(w1), 0, "e4m3").T @ mxq(z, 0, "e4m3") + mxq(f64(w2), 0, "e4m3").T @ x_two
    st = h[np.arange(N)[:, None], runs(n3, N)] - h
    return h * (sigmoid(st[np.arange(N)[:, None], runs(n4, N)]))

@@ -1,0 +1,203 @@
+from contextlib import ExitStack
+
+import concourse.mybir as mybir
+
+F32 = mybir.dt.float32
+BF16 = mybir.dt.bfloat16
+I32 = mybir.dt.int32
+U32 = mybir.dt.uint32
+U16 = mybir.dt.uint16
+U8 = mybir.dt.uint8
+FP8X4 = mybir.dt.float8_e4m3fn_x4
+ALU = mybir.AluOpType
+ACT = mybir.ActivationFunctionType
+
+P = 128
+PACK = 4
+S = 512
+TABLE = 2048
+HALF = S // 2
+FLOPS = 3 * 2 * 512 * 512 * 512
+
+
+def entries(offsets, first, count):
+    return offsets[:, first // 16 : (first + count) // 16]
+
+
+def tile_picked_kmixunderhopd_none_p_kernel(
+    tc, x_words, x_scales, d_words, d_scales, gn, w1, w2, offs, k1, n1, n2, two, n3, n4, out
+):
+    nc = tc.nc
+    with ExitStack() as ctx:
+        keep = ctx.enter_context(tc.tile_pool(name="keep", bufs=1))
+        psum = ctx.enter_context(tc.psum_pool(name="psum", bufs=1))
+
+        def load_list(name, src):
+            tile = keep.tile([P, S // 16], U16, name=name)
+            nc.sync.dma_start(tile[:], src)
+            return tile
+
+        d_byte_table = keep.tile([P, TABLE], U8, name="d_byte_table")
+        x_byte_table = keep.tile([P, TABLE], U8, name="x_byte_table")
+        key_scales = keep.tile([P, S], U8, name="key_scales", align_bytes=64)
+        nc.vector.memset(d_byte_table[:].bitcast(I32), 0)
+        nc.vector.memset(x_byte_table[:].bitcast(I32), 0)
+        nc.gpsimd.memset(key_scales[:].bitcast(I32), 0)
+
+        k1_sb = load_list("k1_sb", k1)
+        d_word_table = keep.tile([P, TABLE], I32, name="d_word_table")
+        nc.sync.dma_start(d_word_table[:], d_words[0].rearrange("p c r -> p (c r)").bitcast(I32))
+        nc.scalar.dma_start(d_byte_table[:].bitcast(I32)[0:P:8, :], d_scales[0].bitcast(I32))
+        offs_sb = load_list("offs_sb", offs)
+        x_word_table = keep.tile([P, TABLE], I32, name="x_word_table")
+        nc.sync.dma_start(x_word_table[:], x_words[0].rearrange("p c r -> p (c r)").bitcast(I32))
+        for q in range(4):
+            nc.scalar.dma_start(
+                x_byte_table[:].bitcast(I32)[32 * q : 32 * q + 4, :], x_scales[0].bitcast(I32)[4 * q : 4 * q + 4, :]
+            )
+        gain = keep.tile([P, PACK], F32, name="gain")
+        nc.gpsimd.dma_start(gain[:], gn.rearrange("(p t) o -> p (t o)", t=PACK))
+
+        key_bytes = keep.tile([P, S], U8, name="key_bytes")
+        nc.vector.tensor_copy(key_bytes[:], d_byte_table[:].indirect(k1_sb[:]))
+        key_bytes_dealt = keep.tile([P, S], U8, name="key_bytes_dealt")
+        nc.vector.tensor_copy(
+            key_bytes_dealt[:].rearrange("p (t m) -> p m t", t=PACK), key_bytes[:].rearrange("p (m t) -> p m t", t=PACK)
+        )
+        for r in range(4):
+            nc.scalar.dma_start(
+                key_scales[:].bitcast(I32)[r:P:32, :], key_bytes_dealt[:].bitcast(I32)[8 * r : P : 32, :]
+            )
+        key_words = keep.tile([P, S], U32, name="key_words")
+        nc.vector.tensor_copy(key_words[:], d_word_table[:].bitcast(U32).indirect(k1_sb[:]))
+        key_codes = keep.tile([P, S], I32, name="key_codes", align_bytes=64)
+        nc.vector.tensor_copy(
+            key_codes[:].rearrange("p (t m) -> p m t", t=PACK),
+            key_words[:].bitcast(I32).rearrange("p (m t) -> p m t", t=PACK),
+        )
+
+        def pick_tokens(name, offsets):
+            scales = keep.tile([P, S], U8, name=name + "_scales", align_bytes=64)
+            nc.vector.tensor_copy(scales[:], x_byte_table[:].indirect(offsets[:]))
+            codes = keep.tile([P, S], U32, name=name + "_codes", align_bytes=64)
+            nc.vector.tensor_copy(codes[:], x_word_table[:].bitcast(U32).indirect(offsets[:]))
+            return codes, scales
+
+        tok_codes, tok_scales = pick_tokens("tok", offs_sb)
+
+        two_sb = load_list("two_sb", two)
+        n1_sb = load_list("n1_sb", n1)
+        n2_sb = load_list("n2_sb", n2)
+        w2_raw = keep.tile([P, PACK, S], F32, name="w2_raw")
+        nc.sync.dma_start(w2_raw[:], w2.rearrange("(p j) c -> p j c", j=PACK))
+        w1_raw = keep.tile([P, PACK, S], F32, name="w1_raw")
+        nc.sync.dma_start(w1_raw[:], w1.rearrange("(p j) c -> p j c", j=PACK))
+        n3_sb = load_list("n3_sb", n3)
+        n4_sb = load_list("n4_sb", n4)
+
+        s_sb = []
+        for t in range(PACK):
+            bank = psum.tile([P, S], F32, name="s_bank%d" % t)
+            cols = slice(P * t, P * (t + 1))
+            nc.tensor.matmul_mx(
+                out=bank[:], lhsT=key_codes[:, cols].bitcast(FP8X4), lhsT_scale=key_scales[:, cols],
+                rhs=tok_codes[:].bitcast(FP8X4), rhs_scale=tok_scales[:], start=True, stop=True,
+            )
+            s_t = keep.tile([P, S], F32, name="s_sb%d" % t)
+            nc.scalar.copy(s_t[:], bank[:])
+            s_sb.append(s_t)
+
+        two_codes, two_scales = pick_tokens("two", two_sb)
+
+        def quantise_weight(name, raw):
+            grouped = keep.tile([P, PACK * S], BF16, name=name + "_grouped", align_bytes=64)
+            nc.vector.tensor_copy(
+                grouped[:].rearrange("p (t m j) -> p m j t", t=PACK, j=PACK),
+                raw[:].rearrange("p j (m t) -> p m j t", t=PACK),
+            )
+            codes = keep.tile([P, S], U32, name=name + "_codes", align_bytes=64)
+            scales = keep.tile([P, S], U8, name=name + "_scales", align_bytes=64)
+            nc.vector.quantize_mx(out=codes[:].bitcast(FP8X4), scales=scales[:], in_=grouped[:])
+            return codes, scales
+
+        h_banks = [psum.tile([P, S], F32, name="h_bank%d" % t) for t in range(PACK)]
+        z_codes = keep.tile([P, S], U32, name="z_codes", align_bytes=64)
+        z_scales = keep.tile([P, S], U8, name="z_scales", align_bytes=64)
+
+        def contrast(half, t, z_planes):
+            first = half * HALF
+            at_n1 = keep.tile([P, HALF], F32, name="at_n1_%d_%d" % (half, t))
+            nc.scalar.activation(at_n1[:], s_sb[t][:].indirect(entries(n1_sb, first, HALF)), ACT.Copy)
+            at_n2 = keep.tile([P, HALF], F32, name="at_n2_%d_%d" % (half, t))
+            nc.scalar.activation(at_n2[:], s_sb[t][:].indirect(entries(n2_sb, first, HALF)), ACT.Copy)
+            least = keep.tile([P, HALF], F32, name="least_%d_%d" % (half, t))
+            nc.vector.tensor_tensor(least[:], at_n1[:], at_n2[:], ALU.min)
+            diff = keep.tile([P, HALF], F32, name="diff_%d_%d" % (half, t))
+            nc.vector.tensor_tensor(diff[:], s_sb[t][:, first : first + HALF], least[:], ALU.subtract)
+            nc.vector.tensor_scalar(z_planes[:, t, :], diff[:], gain[:, t : t + 1], 0.0625, ALU.mult, ALU.mult)
+
+        def quantise_z(half, z_planes):
+            cols = slice(half * HALF, (half + 1) * HALF)
+            grouped = keep.tile([P, HALF, PACK], BF16, name="z_grouped%d" % half, align_bytes=64)
+            nc.vector.tensor_copy(
+                grouped[:].rearrange("p (c i) t -> p c t i", i=4), z_planes[:].rearrange("p t (c i) -> p c t i", i=4)
+            )
+            nc.vector.quantize_mx(
+                out=z_codes[:, cols].bitcast(FP8X4), scales=z_scales[:, cols], in_=grouped[:].rearrange("p c t -> p (c t)")
+            )
+
+        z_planes = [keep.tile([P, PACK, HALF], BF16, name="z_planes%d" % half) for half in range(2)]
+        for t in range(PACK):
+            contrast(0, t, z_planes[0])
+        quantise_z(0, z_planes[0])
+        w2_codes, w2_scales = quantise_weight("w2", w2_raw)
+        for t in range(PACK):
+            rows = slice(P * t, P * (t + 1))
+            nc.tensor.matmul_mx(
+                out=h_banks[t][:], lhsT=w2_codes[:, rows].bitcast(FP8X4), lhsT_scale=w2_scales[:, rows],
+                rhs=two_codes[:].bitcast(FP8X4), rhs_scale=two_scales[:], start=True, stop=False,
+            )
+        w1_codes, w1_scales = quantise_weight("w1", w1_raw)
+        for t in range(PACK):
+            contrast(1, t, z_planes[1])
+        quantise_z(1, z_planes[1])
+        for half in range(2):
+            cols = slice(half * HALF, (half + 1) * HALF)
+            for t in range(PACK):
+                rows = slice(P * t, P * (t + 1))
+                nc.tensor.matmul_mx(
+                    out=h_banks[t][:, cols], lhsT=w1_codes[:, rows].bitcast(FP8X4), lhsT_scale=w1_scales[:, rows],
+                    rhs=z_codes[:, cols].bitcast(FP8X4), rhs_scale=z_scales[:, cols], start=False, stop=(half == 1),
+                )
+
+        out_rows = out.rearrange("(p t) c -> p t c", t=PACK)
+        h_sb = []
+        steps = []
+        for t in range(PACK):
+            h_t = keep.tile([P, S], F32, name="h_sb%d" % t)
+            nc.vector.tensor_copy(h_t[:], h_banks[t][:])
+            h_sb.append(h_t)
+
+        def first_hop(t):
+            step = keep.tile([P, S], F32, name="step%d" % t)
+            for half in range(2):
+                cols = slice(half * HALF, (half + 1) * HALF)
+                at_n3 = keep.tile([P, HALF], F32, name="at_n3_%d_%d" % (half, t))
+                nc.scalar.activation(at_n3[:], h_sb[t][:].indirect(entries(n3_sb, half * HALF, HALF)), ACT.Copy)
+                nc.vector.tensor_tensor(step[:, cols], at_n3[:], h_sb[t][:, cols], ALU.subtract)
+            steps.append(step)
+
+        def second_hop(t):
+            for half in range(2):
+                cols = slice(half * HALF, (half + 1) * HALF)
+                gate = keep.tile([P, HALF], F32, name="gate_%d_%d" % (half, t))
+                nc.scalar.activation(gate[:], steps[t][:].indirect(entries(n4_sb, half * HALF, HALF)), ACT.Sigmoid)
+                result = keep.tile([P, HALF], F32, name="result_%d_%d" % (half, t))
+                nc.vector.tensor_tensor(result[:], gate[:], h_sb[t][:, cols], ALU.mult)
+                nc.sync.dma_start(out_rows[:, t, cols], result[:])
+
+        first_hop(0)
+        for t in range(1, PACK):
+            first_hop(t)
+            second_hop(t - 1)
+        second_hop(PACK - 1)

@@ -18,6 +18,9 @@ S = 512
 TABLE = 2048
 HALF = S // 2
 FLOPS = 3 * 2 * 512 * 512 * 512
+S_COPY_ON_VECTOR = (1,)
+FUSED_TILES = (0, 1)
+SPARE = 32
 
 
 def entries(offsets, first, count):
@@ -37,26 +40,36 @@ def tile_picked_kmixunderhopd_none_p_kernel(
             nc.sync.dma_start(tile[:], src)
             return tile
 
-        d_byte_table = keep.tile([P, TABLE], U8, name="d_byte_table")
         x_byte_table = keep.tile([P, TABLE], U8, name="x_byte_table")
-        key_scales = keep.tile([P, S], U8, name="key_scales", align_bytes=64)
-        nc.vector.memset(d_byte_table[:].bitcast(I32), 0)
-        nc.vector.memset(x_byte_table[:].bitcast(I32), 0)
-        nc.gpsimd.memset(key_scales[:].bitcast(I32), 0)
+        warm_in = keep.tile([P, 1], F32, name="warm_in")
+        warm_out = keep.tile([P, 1], F32, name="warm_out")
+        nc.gpsimd.memset(warm_in[:], 0.0)
+        nc.scalar.activation(warm_out[:], warm_in[:], ACT.Sigmoid)
 
         k1_sb = load_list("k1_sb", k1)
-        d_word_table = keep.tile([P, TABLE], I32, name="d_word_table")
-        nc.sync.dma_start(d_word_table[:], d_words[0].rearrange("p c r -> p (c r)").bitcast(I32))
-        nc.scalar.dma_start(d_byte_table[:].bitcast(I32)[0:P:8, :], d_scales[0].bitcast(I32))
+        d_byte_table = keep.tile([P, TABLE], U8, name="d_byte_table")
+        nc.sync.dma_start(
+            d_byte_table[:].bitcast(I32), d_scales[0].bitcast(I32).unsqueeze(1).to_broadcast([16, 8, TABLE // 4])
+        )
+        for q in range(4):
+            nc.sync.dma_start(
+                x_byte_table[:].bitcast(I32)[32 * q : 32 * q + 32, :],
+                x_scales[0].bitcast(I32)[4 * q : 4 * q + 4, :].unsqueeze(0).to_broadcast([8, 4, TABLE // 4]),
+            )
         offs_sb = load_list("offs_sb", offs)
+        d_word_table = keep.tile([P, TABLE], I32, name="d_word_table", tag="d_words_then_w2")
+        nc.sync.dma_start(d_word_table[:], d_words[0].rearrange("p c r -> p (c r)").bitcast(I32))
+        n1_sb = load_list("n1_sb", n1)
+        n2_sb = load_list("n2_sb", n2)
         x_word_table = keep.tile([P, TABLE], I32, name="x_word_table")
         nc.sync.dma_start(x_word_table[:], x_words[0].rearrange("p c r -> p (c r)").bitcast(I32))
-        for q in range(4):
-            nc.scalar.dma_start(
-                x_byte_table[:].bitcast(I32)[32 * q : 32 * q + 4, :], x_scales[0].bitcast(I32)[4 * q : 4 * q + 4, :]
-            )
+        two_sb = load_list("two_sb", two)
+        n3_sb = load_list("n3_sb", n3)
+        n4_sb = load_list("n4_sb", n4)
         gain = keep.tile([P, PACK], F32, name="gain")
         nc.gpsimd.dma_start(gain[:], gn.rearrange("(p t) o -> p (t o)", t=PACK))
+        minus_gain = keep.tile([P, PACK], F32, name="minus_gain")
+        nc.gpsimd.tensor_scalar(minus_gain[:], gain[:], -1.0, 0.0, ALU.mult, ALU.add)
 
         key_bytes = keep.tile([P, S], U8, name="key_bytes")
         nc.vector.tensor_copy(key_bytes[:], d_byte_table[:].indirect(k1_sb[:]))
@@ -64,140 +77,178 @@ def tile_picked_kmixunderhopd_none_p_kernel(
         nc.vector.tensor_copy(
             key_bytes_dealt[:].rearrange("p (t m) -> p m t", t=PACK), key_bytes[:].rearrange("p (m t) -> p m t", t=PACK)
         )
-        for r in range(4):
+        key_scales = keep.tile([P, S], U8, name="key_scales", align_bytes=64)
+        nc.vector.tensor_copy(key_scales[:].bitcast(I32), key_bytes_dealt[:].bitcast(I32))
+        for r in range(1, 4):
             nc.scalar.dma_start(
                 key_scales[:].bitcast(I32)[r:P:32, :], key_bytes_dealt[:].bitcast(I32)[8 * r : P : 32, :]
             )
-        key_words = keep.tile([P, S], U32, name="key_words")
+
+        def pick_scales(name, offsets):
+            scales = keep.tile([P, S], U8, name=name + "_scales", align_bytes=64)
+            nc.vector.tensor_copy(scales[:], x_byte_table[:].indirect(offsets[:]))
+            return scales
+
+        def pick_codes(name, offsets):
+            codes = keep.tile([P, S], U32, name=name + "_codes", align_bytes=64)
+            nc.vector.tensor_copy(codes[:], x_word_table[:].bitcast(U32).indirect(offsets[:]))
+            return codes
+
+        tok_scales = pick_scales("tok", offs_sb)
+        key_words = keep.tile([P, S], U32, name="key_words", tag="key_words_then_w1")
         nc.vector.tensor_copy(key_words[:], d_word_table[:].bitcast(U32).indirect(k1_sb[:]))
         key_codes = keep.tile([P, S], I32, name="key_codes", align_bytes=64)
         nc.vector.tensor_copy(
             key_codes[:].rearrange("p (t m) -> p m t", t=PACK),
             key_words[:].bitcast(I32).rearrange("p (m t) -> p m t", t=PACK),
         )
+        tok_codes = pick_codes("tok", offs_sb)
 
-        def pick_tokens(name, offsets):
-            scales = keep.tile([P, S], U8, name=name + "_scales", align_bytes=64)
-            nc.vector.tensor_copy(scales[:], x_byte_table[:].indirect(offsets[:]))
-            codes = keep.tile([P, S], U32, name=name + "_codes", align_bytes=64)
-            nc.vector.tensor_copy(codes[:], x_word_table[:].bitcast(U32).indirect(offsets[:]))
-            return codes, scales
-
-        tok_codes, tok_scales = pick_tokens("tok", offs_sb)
-
-        two_sb = load_list("two_sb", two)
-        n1_sb = load_list("n1_sb", n1)
-        n2_sb = load_list("n2_sb", n2)
-        w2_raw = keep.tile([P, PACK, S], F32, name="w2_raw")
+        w2_raw = keep.tile([P, PACK, S], F32, name="w2_raw", tag="d_words_then_w2")
         nc.sync.dma_start(w2_raw[:], w2.rearrange("(p j) c -> p j c", j=PACK))
-        w1_raw = keep.tile([P, PACK, S], F32, name="w1_raw")
+        w1_raw = keep.tile([P, PACK, S], F32, name="w1_raw", tag="key_words_then_w1")
         nc.sync.dma_start(w1_raw[:], w1.rearrange("(p j) c -> p j c", j=PACK))
-        n3_sb = load_list("n3_sb", n3)
-        n4_sb = load_list("n4_sb", n4)
 
         s_sb = []
         for t in range(PACK):
-            bank = psum.tile([P, S], F32, name="s_bank%d" % t)
+            s_t = keep.tile([P, S + SPARE], F32, name="s_sb%d" % t)
+            nc.gpsimd.memset(s_t[:, S:], 0.0)
+            s_sb.append(s_t)
+        for t in range(PACK):
+            bank = psum.tile([P, S], F32, name="s_bank%d" % t, tag="bank%d" % t)
             cols = slice(P * t, P * (t + 1))
             nc.tensor.matmul_mx(
                 out=bank[:], lhsT=key_codes[:, cols].bitcast(FP8X4), lhsT_scale=key_scales[:, cols],
                 rhs=tok_codes[:].bitcast(FP8X4), rhs_scale=tok_scales[:], start=True, stop=True,
             )
-            s_t = keep.tile([P, S], F32, name="s_sb%d" % t)
-            nc.scalar.copy(s_t[:], bank[:])
-            s_sb.append(s_t)
+            if t in S_COPY_ON_VECTOR:
+                nc.vector.tensor_scalar(s_sb[t][:, 0:S], bank[:], 0.0625, None, ALU.mult)
+            else:
+                nc.scalar.activation(s_sb[t][:, 0:S], bank[:], ACT.Copy, scale=0.0625)
 
-        two_codes, two_scales = pick_tokens("two", two_sb)
+        two_scales = pick_scales("two", two_sb)
+        two_codes = pick_codes("two", two_sb)
 
-        def quantise_weight(name, raw):
-            grouped = keep.tile([P, PACK * S], BF16, name=name + "_grouped", align_bytes=64)
-            nc.vector.tensor_copy(
-                grouped[:].rearrange("p (t m j) -> p m j t", t=PACK, j=PACK),
-                raw[:].rearrange("p j (m t) -> p m j t", t=PACK),
+        w_codes = [keep.tile([P, S], U32, name="w_codes0", align_bytes=64)]
+        w_scales = [keep.tile([P, S], U8, name="w_scales%d" % pair, align_bytes=64) for pair in range(2)]
+        w_raw = [w2_raw, w1_raw]
+
+        def round_weight(i, pair, grouped, round_copy):
+            round_copy(
+                grouped.rearrange("p (t a b j) -> p a t j b", a=16, b=8, j=PACK),
+                w_raw[i][:].rearrange("p j (a t b) -> p a t j b", a=16, b=8)[:, :, 2 * pair : 2 * pair + 2, :, :],
             )
-            codes = keep.tile([P, S], U32, name=name + "_codes", align_bytes=64)
-            scales = keep.tile([P, S], U8, name=name + "_scales", align_bytes=64)
-            nc.vector.quantize_mx(out=codes[:].bitcast(FP8X4), scales=scales[:], in_=grouped[:])
-            return codes, scales
 
-        h_banks = [psum.tile([P, S], F32, name="h_bank%d" % t) for t in range(PACK)]
+        def early_weight(i, tag):
+            grouped = keep.tile([P, 2 * S], BF16, name="w_grouped", tag=tag, align_bytes=64)
+            round_weight(i, 0, grouped[:], nc.vector.tensor_copy)
+            cols = slice(2 * P * i, 2 * P * (i + 1))
+            nc.vector.quantize_mx(out=w_codes[0][:, cols].bitcast(FP8X4), scales=w_scales[0][:, cols], in_=grouped[:])
+
         z_codes = keep.tile([P, S], U32, name="z_codes", align_bytes=64)
         z_scales = keep.tile([P, S], U8, name="z_scales", align_bytes=64)
+        z_planes = keep.tile([P, PACK, S], BF16, name="z_planes")
+        h_window = [keep.tile([P, 2 * S], F32, name="h_window%d" % t) for t in range(PACK)]
+        second_window = [keep.tile([P, 2 * S], F32, name="second_window%d" % t) for t in range(PACK)]
 
-        def contrast(half, t, z_planes):
-            first = half * HALF
-            at_n1 = keep.tile([P, HALF], F32, name="at_n1_%d_%d" % (half, t))
-            nc.scalar.activation(at_n1[:], s_sb[t][:].indirect(entries(n1_sb, first, HALF)), ACT.Copy)
-            at_n2 = keep.tile([P, HALF], F32, name="at_n2_%d_%d" % (half, t))
-            nc.scalar.activation(at_n2[:], s_sb[t][:].indirect(entries(n2_sb, first, HALF)), ACT.Copy)
-            least = keep.tile([P, HALF], F32, name="least_%d_%d" % (half, t))
-            nc.vector.tensor_tensor(least[:], at_n1[:], at_n2[:], ALU.min)
-            diff = keep.tile([P, HALF], F32, name="diff_%d_%d" % (half, t))
-            nc.vector.tensor_tensor(diff[:], s_sb[t][:, first : first + HALF], least[:], ALU.subtract)
-            nc.vector.tensor_scalar(z_planes[:, t, :], diff[:], gain[:, t : t + 1], 0.0625, ALU.mult, ALU.mult)
+        gained = [keep.tile([P, S], F32, name="gained", tag="gained%d" % t, align_bytes=64) for t in range(PACK)]
 
-        def quantise_z(half, z_planes):
+        def gain_scores(t):
+            nc.vector.tensor_scalar(gained[t][:], s_sb[t][:, 0:S], gain[:, t : t + 1], None, ALU.mult)
+
+        def contrast(t, first, count, tag):
+            cols = slice(first, first + count)
+            at_n1 = h_window[t][:, S + first : S + first + count]
+            nc.scalar.activation(at_n1, s_sb[t][:].indirect(entries(n1_sb, first, count)), ACT.Copy)
+            at_n2 = second_window[t][:, S + first : S + first + count]
+            nc.scalar.activation(at_n2, s_sb[t][:].indirect(entries(n2_sb, first, count)), ACT.Copy)
+            least = keep.tile([P, count], F32, name="least", tag=tag, align_bytes=64)
+            nc.vector.tensor_tensor(least[:], at_n1, at_n2, ALU.min)
+            nc.vector.scalar_tensor_tensor(
+                z_planes[:, t, cols], least[:], minus_gain[:, t : t + 1], gained[t][:, cols], ALU.mult, ALU.add
+            )
+
+        def quantise_z(half):
             cols = slice(half * HALF, (half + 1) * HALF)
-            grouped = keep.tile([P, HALF, PACK], BF16, name="z_grouped%d" % half, align_bytes=64)
+            grouped = keep.tile([P, HALF, PACK], BF16, name="z_grouped", tag="z_grouped%d" % half, align_bytes=64)
             nc.vector.tensor_copy(
-                grouped[:].rearrange("p (c i) t -> p c t i", i=4), z_planes[:].rearrange("p t (c i) -> p c t i", i=4)
+                grouped[:].rearrange("p (c i) t -> p c t i", i=4),
+                z_planes[:, :, cols].rearrange("p t (c i) -> p c t i", i=4),
             )
             nc.vector.quantize_mx(
                 out=z_codes[:, cols].bitcast(FP8X4), scales=z_scales[:, cols], in_=grouped[:].rearrange("p c t -> p (c t)")
             )
 
-        z_planes = [keep.tile([P, PACK, HALF], BF16, name="z_planes%d" % half) for half in range(2)]
-        for t in range(PACK):
-            contrast(0, t, z_planes[0])
-        quantise_z(0, z_planes[0])
-        w2_codes, w2_scales = quantise_weight("w2", w2_raw)
-        for t in range(PACK):
-            rows = slice(P * t, P * (t + 1))
-            nc.tensor.matmul_mx(
-                out=h_banks[t][:], lhsT=w2_codes[:, rows].bitcast(FP8X4), lhsT_scale=w2_scales[:, rows],
-                rhs=two_codes[:].bitcast(FP8X4), rhs_scale=two_scales[:], start=True, stop=False,
-            )
-        w1_codes, w1_scales = quantise_weight("w1", w1_raw)
-        for t in range(PACK):
-            contrast(1, t, z_planes[1])
-        quantise_z(1, z_planes[1])
+        early_weight(0, "w2_then_least")
+        gain_scores(0)
+        contrast(0, 0, S, "w2_then_least")
+        gain_scores(1)
+        early_weight(1, "w1_then_least")
+        contrast(1, 0, S, "w1_then_least")
+        gain_scores(2)
+        gain_scores(3)
         for half in range(2):
-            cols = slice(half * HALF, (half + 1) * HALF)
-            for t in range(PACK):
-                rows = slice(P * t, P * (t + 1))
+            for t in (2, 3):
+                contrast(t, half * HALF, HALF, "w1_then_least")
+            quantise_z(half)
+        late_grouped = keep.tile([P, 4 * S], BF16, name="late_grouped", tag="late_grouped", align_bytes=64)
+        for i in range(2):
+            round_weight(i, 1, late_grouped[:, 2 * S * i : 2 * S * (i + 1)], nc.scalar.copy)
+
+        def project(bank, t, cols):
+            for i, (moving, moving_scales) in enumerate(((two_codes, two_scales), (z_codes, z_scales))):
+                rows = slice(P * (2 * i + t % 2), P * (2 * i + t % 2 + 1))
                 nc.tensor.matmul_mx(
-                    out=h_banks[t][:, cols], lhsT=w1_codes[:, rows].bitcast(FP8X4), lhsT_scale=w1_scales[:, rows],
-                    rhs=z_codes[:, cols].bitcast(FP8X4), rhs_scale=z_scales[:, cols], start=False, stop=(half == 1),
+                    out=bank[:], lhsT=w_codes[t // 2][:, rows].bitcast(FP8X4), lhsT_scale=w_scales[t // 2][:, rows],
+                    rhs=moving[:, cols].bitcast(FP8X4), rhs_scale=moving_scales[:, cols], start=(i == 0), stop=(i == 1),
                 )
 
-        out_rows = out.rearrange("(p t) c -> p t c", t=PACK)
-        h_sb = []
-        steps = []
-        for t in range(PACK):
-            h_t = keep.tile([P, S], F32, name="h_sb%d" % t)
-            nc.vector.tensor_copy(h_t[:], h_banks[t][:])
-            h_sb.append(h_t)
+        def h_part(t, first, count, tag, leave_bank):
+            bank = psum.tile([P, count], F32, name="h_bank", tag=tag)
+            project(bank, t, slice(first, first + count))
+            leave_bank(h_window[t][:, first : first + count], bank[:])
 
-        def first_hop(t):
-            step = keep.tile([P, S], F32, name="step%d" % t)
-            for half in range(2):
-                cols = slice(half * HALF, (half + 1) * HALF)
-                at_n3 = keep.tile([P, HALF], F32, name="at_n3_%d_%d" % (half, t))
-                nc.scalar.activation(at_n3[:], h_sb[t][:].indirect(entries(n3_sb, half * HALF, HALF)), ACT.Copy)
-                nc.vector.tensor_tensor(step[:, cols], at_n3[:], h_sb[t][:, cols], ALU.subtract)
-            steps.append(step)
+        out_rows = out.rearrange("(a t b) c -> t a b c", a=16, b=8)
 
-        def second_hop(t):
-            for half in range(2):
-                cols = slice(half * HALF, (half + 1) * HALF)
-                gate = keep.tile([P, HALF], F32, name="gate_%d_%d" % (half, t))
-                nc.scalar.activation(gate[:], steps[t][:].indirect(entries(n4_sb, half * HALF, HALF)), ACT.Sigmoid)
-                result = keep.tile([P, HALF], F32, name="result_%d_%d" % (half, t))
-                nc.vector.tensor_tensor(result[:], gate[:], h_sb[t][:, cols], ALU.mult)
-                nc.sync.dma_start(out_rows[:, t, cols], result[:])
+        def first_hop(t, count):
+            if t in FUSED_TILES:
+                step = keep.tile([P, S], F32, name="step%d" % t)
+            else:
+                step = second_window[t]
+            for first in range(0, S, count):
+                cols = slice(first, first + count)
+                at_n3 = keep.tile([P, count], F32, name="at_n3_%d_%d" % (t, first))
+                nc.scalar.activation(at_n3[:], h_window[t][:].indirect(entries(n3_sb, first, count)), ACT.Copy)
+                nc.vector.tensor_tensor(step[:, cols], at_n3[:], h_window[t][:, cols], ALU.subtract)
+            if t in FUSED_TILES:
+                nc.scalar.activation(second_window[t][:, 0:S], step[:], ACT.Sigmoid)
 
-        first_hop(0)
-        for t in range(1, PACK):
-            first_hop(t)
-            second_hop(t - 1)
-        second_hop(PACK - 1)
+        def second_hop(t, count):
+            for first in range(0, S, count):
+                cols = slice(first, first + count)
+                looked_up = second_window[t][:].indirect(entries(n4_sb, first, count))
+                result = keep.tile([P, count], F32, name="result_%d_%d" % (t, first))
+                if t in FUSED_TILES:
+                    nc.vector.tensor_tensor(result[:], looked_up, h_window[t][:, cols], ALU.mult)
+                else:
+                    gate = keep.tile([P, count], F32, name="gate_%d_%d" % (t, first))
+                    nc.scalar.activation(gate[:], looked_up, ACT.Sigmoid)
+                    nc.vector.tensor_tensor(result[:], gate[:], h_window[t][:, cols], ALU.mult)
+                nc.sync.dma_start(out_rows[t][:, :, cols], result[:])
+
+        for t in range(2):
+            h_part(t, 0, HALF, "h_low%d" % t, nc.scalar.copy)
+        for t in range(2):
+            h_part(t, HALF, HALF, "h_high%d" % t, nc.vector.tensor_copy if t else nc.scalar.copy)
+        w_codes.append(keep.tile([P, S], U32, name="w_codes1", tag="z_grouped1", align_bytes=64))
+        nc.vector.quantize_mx(out=w_codes[1][:].bitcast(FP8X4), scales=w_scales[1][:], in_=late_grouped[:])
+        first_hop(0, S)
+        h_part(2, 0, S, "bank2", nc.vector.tensor_copy)
+        first_hop(1, S)
+        h_part(3, 0, S, "bank3", nc.vector.tensor_copy)
+        first_hop(2, S)
+        second_hop(0, S)
+        first_hop(3, HALF)
+        second_hop(1, S)
+        second_hop(2, S)
+        second_hop(3, HALF)

@@ -18,8 +18,8 @@ S = 512
 TABLE = 2048
 HALF = S // 2
 FLOPS = 3 * 2 * 512 * 512 * 512
-S_COPY_ON_VECTOR = (1,)
-FUSED_TILES = (0, 1)
+S_COPY_ON_VECTOR = ()
+FUSED_TILES = (0,)
 SPARE = 32
 
 
@@ -75,7 +75,7 @@ def tile_picked_kmixunderhopd_none_p_kernel(
         nc.vector.tensor_copy(key_bytes[:], d_byte_table[:].indirect(k1_sb[:]))
         key_bytes_dealt = keep.tile([P, S], U8, name="key_bytes_dealt")
         nc.vector.tensor_copy(
-            key_bytes_dealt[:].rearrange("p (t m) -> p m t", t=PACK), key_bytes[:].rearrange("p (m t) -> p m t", t=PACK)
+            key_bytes_dealt[:].rearrange("p (t m) -> p t m", t=PACK), key_bytes[:].rearrange("p (m t) -> p t m", t=PACK)
         )
         key_scales = keep.tile([P, S], U8, name="key_scales", align_bytes=64)
         nc.vector.tensor_copy(key_scales[:].bitcast(I32), key_bytes_dealt[:].bitcast(I32))
@@ -189,7 +189,7 @@ def tile_picked_kmixunderhopd_none_p_kernel(
         gain_scores(3)
         for half in range(2):
             for t in (2, 3):
-                contrast(t, half * HALF, HALF, "w1_then_least")
+                contrast(t, half * HALF, HALF, "gained1" if t == 2 else "w1_then_least")
             quantise_z(half)
         late_grouped = keep.tile([P, 4 * S], BF16, name="late_grouped", tag="late_grouped", align_bytes=64)
         for i in range(2):
@@ -248,7 +248,7 @@ def tile_picked_kmixunderhopd_none_p_kernel(
         h_part(3, 0, S, "bank3", nc.vector.tensor_copy)
         first_hop(2, S)
         second_hop(0, S)
-        first_hop(3, HALF)
         second_hop(1, S)
+        first_hop(3, HALF)
         second_hop(2, S)
         second_hop(3, HALF)

from contextlib import ExitStack

import concourse.mybir as mybir

F32 = mybir.dt.float32
BF16 = mybir.dt.bfloat16
I32 = mybir.dt.int32
U32 = mybir.dt.uint32
U16 = mybir.dt.uint16
U8 = mybir.dt.uint8
FP8X4 = mybir.dt.float8_e4m3fn_x4
ALU = mybir.AluOpType
ACT = mybir.ActivationFunctionType

P = 128
PACK = 4
S = 512
TABLE = 2048
HALF = S // 2
FLOPS = 3 * 2 * 512 * 512 * 512
S_COPY_ON_VECTOR = ()
FUSED_TILES = (0,)
SPARE = 32


def entries(offsets, first, count):
    return offsets[:, first // 16 : (first + count) // 16]


def tile_picked_kmixunderhopd_none_p_kernel(
    tc, x_words, x_scales, d_words, d_scales, gn, w1, w2, offs, k1, n1, n2, two, n3, n4, out
):
    nc = tc.nc
    with ExitStack() as ctx:
        keep = ctx.enter_context(tc.tile_pool(name="keep", bufs=1))
        psum = ctx.enter_context(tc.psum_pool(name="psum", bufs=1))

        def load_list(name, src):
            tile = keep.tile([P, S // 16], U16, name=name)
            nc.sync.dma_start(tile[:], src)
            return tile

        x_byte_table = keep.tile([P, TABLE], U8, name="x_byte_table")
        warm_in = keep.tile([P, 1], F32, name="warm_in")
        warm_out = keep.tile([P, 1], F32, name="warm_out")
        nc.gpsimd.memset(warm_in[:], 0.0)
        nc.scalar.activation(warm_out[:], warm_in[:], ACT.Sigmoid)

        k1_sb = load_list("k1_sb", k1)
        d_byte_table = keep.tile([P, TABLE], U8, name="d_byte_table")
        nc.sync.dma_start(
            d_byte_table[:].bitcast(I32), d_scales[0].bitcast(I32).unsqueeze(1).to_broadcast([16, 8, TABLE // 4])
        )
        for q in range(4):
            nc.sync.dma_start(
                x_byte_table[:].bitcast(I32)[32 * q : 32 * q + 32, :],
                x_scales[0].bitcast(I32)[4 * q : 4 * q + 4, :].unsqueeze(0).to_broadcast([8, 4, TABLE // 4]),
            )
        offs_sb = load_list("offs_sb", offs)
        d_word_table = keep.tile([P, TABLE], I32, name="d_word_table", tag="d_words_then_w2")
        nc.sync.dma_start(d_word_table[:], d_words[0].rearrange("p c r -> p (c r)").bitcast(I32))
        n1_sb = load_list("n1_sb", n1)
        n2_sb = load_list("n2_sb", n2)
        x_word_table = keep.tile([P, TABLE], I32, name="x_word_table")
        nc.sync.dma_start(x_word_table[:], x_words[0].rearrange("p c r -> p (c r)").bitcast(I32))
        two_sb = load_list("two_sb", two)
        n3_sb = load_list("n3_sb", n3)
        n4_sb = load_list("n4_sb", n4)
        gain = keep.tile([P, PACK], F32, name="gain")
        nc.gpsimd.dma_start(gain[:], gn.rearrange("(p t) o -> p (t o)", t=PACK))
        minus_gain = keep.tile([P, PACK], F32, name="minus_gain")
        nc.gpsimd.tensor_scalar(minus_gain[:], gain[:], -1.0, 0.0, ALU.mult, ALU.add)

        key_bytes = keep.tile([P, S], U8, name="key_bytes")
        nc.vector.tensor_copy(key_bytes[:], d_byte_table[:].indirect(k1_sb[:]))
        key_bytes_dealt = keep.tile([P, S], U8, name="key_bytes_dealt")
        nc.vector.tensor_copy(
            key_bytes_dealt[:].rearrange("p (t m) -> p t m", t=PACK), key_bytes[:].rearrange("p (m t) -> p t m", t=PACK)
        )
        key_scales = keep.tile([P, S], U8, name="key_scales", align_bytes=64)
        nc.vector.tensor_copy(key_scales[:].bitcast(I32), key_bytes_dealt[:].bitcast(I32))
        for r in range(1, 4):
            nc.scalar.dma_start(
                key_scales[:].bitcast(I32)[r:P:32, :], key_bytes_dealt[:].bitcast(I32)[8 * r : P : 32, :]
            )

        def pick_scales(name, offsets):
            scales = keep.tile([P, S], U8, name=name + "_scales", align_bytes=64)
            nc.vector.tensor_copy(scales[:], x_byte_table[:].indirect(offsets[:]))
            return scales

        def pick_codes(name, offsets):
            codes = keep.tile([P, S], U32, name=name + "_codes", align_bytes=64)
            nc.vector.tensor_copy(codes[:], x_word_table[:].bitcast(U32).indirect(offsets[:]))
            return codes

        tok_scales = pick_scales("tok", offs_sb)
        key_words = keep.tile([P, S], U32, name="key_words", tag="key_words_then_w1")
        nc.vector.tensor_copy(key_words[:], d_word_table[:].bitcast(U32).indirect(k1_sb[:]))
        key_codes = keep.tile([P, S], I32, name="key_codes", align_bytes=64)
        nc.vector.tensor_copy(
            key_codes[:].rearrange("p (t m) -> p m t", t=PACK),
            key_words[:].bitcast(I32).rearrange("p (m t) -> p m t", t=PACK),
        )
        tok_codes = pick_codes("tok", offs_sb)

        w2_raw = keep.tile([P, PACK, S], F32, name="w2_raw", tag="d_words_then_w2")
        nc.sync.dma_start(w2_raw[:], w2.rearrange("(p j) c -> p j c", j=PACK))
        w1_raw = keep.tile([P, PACK, S], F32, name="w1_raw", tag="key_words_then_w1")
        nc.sync.dma_start(w1_raw[:], w1.rearrange("(p j) c -> p j c", j=PACK))

        s_sb = []
        for t in range(PACK):
            s_t = keep.tile([P, S + SPARE], F32, name="s_sb%d" % t)
            nc.gpsimd.memset(s_t[:, S:], 0.0)
            s_sb.append(s_t)
        for t in range(PACK):
            bank = psum.tile([P, S], F32, name="s_bank%d" % t, tag="bank%d" % t)
            cols = slice(P * t, P * (t + 1))
            nc.tensor.matmul_mx(
                out=bank[:], lhsT=key_codes[:, cols].bitcast(FP8X4), lhsT_scale=key_scales[:, cols],
                rhs=tok_codes[:].bitcast(FP8X4), rhs_scale=tok_scales[:], start=True, stop=True,
            )
            if t in S_COPY_ON_VECTOR:
                nc.vector.tensor_scalar(s_sb[t][:, 0:S], bank[:], 0.0625, None, ALU.mult)
            else:
                nc.scalar.activation(s_sb[t][:, 0:S], bank[:], ACT.Copy, scale=0.0625)

        two_scales = pick_scales("two", two_sb)
        two_codes = pick_codes("two", two_sb)

        w_codes = [keep.tile([P, S], U32, name="w_codes0", align_bytes=64)]
        w_scales = [keep.tile([P, S], U8, name="w_scales%d" % pair, align_bytes=64) for pair in range(2)]
        w_raw = [w2_raw, w1_raw]

        def round_weight(i, pair, grouped, round_copy):
            round_copy(
                grouped.rearrange("p (t a b j) -> p a t j b", a=16, b=8, j=PACK),
                w_raw[i][:].rearrange("p j (a t b) -> p a t j b", a=16, b=8)[:, :, 2 * pair : 2 * pair + 2, :, :],
            )

        def early_weight(i, tag):
            grouped = keep.tile([P, 2 * S], BF16, name="w_grouped", tag=tag, align_bytes=64)
            round_weight(i, 0, grouped[:], nc.vector.tensor_copy)
            cols = slice(2 * P * i, 2 * P * (i + 1))
            nc.vector.quantize_mx(out=w_codes[0][:, cols].bitcast(FP8X4), scales=w_scales[0][:, cols], in_=grouped[:])

        z_codes = keep.tile([P, S], U32, name="z_codes", align_bytes=64)
        z_scales = keep.tile([P, S], U8, name="z_scales", align_bytes=64)
        z_planes = keep.tile([P, PACK, S], BF16, name="z_planes")
        h_window = [keep.tile([P, 2 * S], F32, name="h_window%d" % t) for t in range(PACK)]
        second_window = [keep.tile([P, 2 * S], F32, name="second_window%d" % t) for t in range(PACK)]

        gained = [keep.tile([P, S], F32, name="gained", tag="gained%d" % t, align_bytes=64) for t in range(PACK)]

        def gain_scores(t):
            nc.vector.tensor_scalar(gained[t][:], s_sb[t][:, 0:S], gain[:, t : t + 1], None, ALU.mult)

        def contrast(t, first, count, tag):
            cols = slice(first, first + count)
            at_n1 = h_window[t][:, S + first : S + first + count]
            nc.scalar.activation(at_n1, s_sb[t][:].indirect(entries(n1_sb, first, count)), ACT.Copy)
            at_n2 = second_window[t][:, S + first : S + first + count]
            nc.scalar.activation(at_n2, s_sb[t][:].indirect(entries(n2_sb, first, count)), ACT.Copy)
            least = keep.tile([P, count], F32, name="least", tag=tag, align_bytes=64)
            nc.vector.tensor_tensor(least[:], at_n1, at_n2, ALU.min)
            nc.vector.scalar_tensor_tensor(
                z_planes[:, t, cols], least[:], minus_gain[:, t : t + 1], gained[t][:, cols], ALU.mult, ALU.add
            )

        def quantise_z(half):
            cols = slice(half * HALF, (half + 1) * HALF)
            grouped = keep.tile([P, HALF, PACK], BF16, name="z_grouped", tag="z_grouped%d" % half, align_bytes=64)
            nc.vector.tensor_copy(
                grouped[:].rearrange("p (c i) t -> p c t i", i=4),
                z_planes[:, :, cols].rearrange("p t (c i) -> p c t i", i=4),
            )
            nc.vector.quantize_mx(
                out=z_codes[:, cols].bitcast(FP8X4), scales=z_scales[:, cols], in_=grouped[:].rearrange("p c t -> p (c t)")
            )

        early_weight(0, "w2_then_least")
        gain_scores(0)
        contrast(0, 0, S, "w2_then_least")
        gain_scores(1)
        early_weight(1, "w1_then_least")
        contrast(1, 0, S, "w1_then_least")
        gain_scores(2)
        gain_scores(3)
        for half in range(2):
            for t in (2, 3):
                contrast(t, half * HALF, HALF, "gained1" if t == 2 else "w1_then_least")
            quantise_z(half)
        late_grouped = keep.tile([P, 4 * S], BF16, name="late_grouped", tag="late_grouped", align_bytes=64)
        for i in range(2):
            round_weight(i, 1, late_grouped[:, 2 * S * i : 2 * S * (i + 1)], nc.scalar.copy)

        def project(bank, t, cols):
            for i, (moving, moving_scales) in enumerate(((two_codes, two_scales), (z_codes, z_scales))):
                rows = slice(P * (2 * i + t % 2), P * (2 * i + t % 2 + 1))
                nc.tensor.matmul_mx(
                    out=bank[:], lhsT=w_codes[t // 2][:, rows].bitcast(FP8X4), lhsT_scale=w_scales[t // 2][:, rows],
                    rhs=moving[:, cols].bitcast(FP8X4), rhs_scale=moving_scales[:, cols], start=(i == 0), stop=(i == 1),
                )

        def h_part(t, first, count, tag, leave_bank):
            bank = psum.tile([P, count], F32, name="h_bank", tag=tag)
            project(bank, t, slice(first, first + count))
            leave_bank(h_window[t][:, first : first + count], bank[:])

        out_rows = out.rearrange("(a t b) c -> t a b c", a=16, b=8)

        def first_hop(t, count):
            if t in FUSED_TILES:
                step = keep.tile([P, S], F32, name="step%d" % t)
            else:
                step = second_window[t]
            for first in range(0, S, count):
                cols = slice(first, first + count)
                at_n3 = keep.tile([P, count], F32, name="at_n3_%d_%d" % (t, first))
                nc.scalar.activation(at_n3[:], h_window[t][:].indirect(entries(n3_sb, first, count)), ACT.Copy)
                nc.vector.tensor_tensor(step[:, cols], at_n3[:], h_window[t][:, cols], ALU.subtract)
            if t in FUSED_TILES:
                nc.scalar.activation(second_window[t][:, 0:S], step[:], ACT.Sigmoid)

        def second_hop(t, count):
            for first in range(0, S, count):
                cols = slice(first, first + count)
                looked_up = second_window[t][:].indirect(entries(n4_sb, first, count))
                result = keep.tile([P, count], F32, name="result_%d_%d" % (t, first))
                if t in FUSED_TILES:
                    nc.vector.tensor_tensor(result[:], looked_up, h_window[t][:, cols], ALU.mult)
                else:
                    gate = keep.tile([P, count], F32, name="gate_%d_%d" % (t, first))
                    nc.scalar.activation(gate[:], looked_up, ACT.Sigmoid)
                    nc.vector.tensor_tensor(result[:], gate[:], h_window[t][:, cols], ALU.mult)
                nc.sync.dma_start(out_rows[t][:, :, cols], result[:])

        for t in range(2):
            h_part(t, 0, HALF, "h_low%d" % t, nc.scalar.copy)
        for t in range(2):
            h_part(t, HALF, HALF, "h_high%d" % t, nc.vector.tensor_copy if t else nc.scalar.copy)
        w_codes.append(keep.tile([P, S], U32, name="w_codes1", tag="z_grouped1", align_bytes=64))
        nc.vector.quantize_mx(out=w_codes[1][:].bitcast(FP8X4), scales=w_scales[1][:], in_=late_grouped[:])
        first_hop(0, S)
        h_part(2, 0, S, "bank2", nc.vector.tensor_copy)
        first_hop(1, S)
        h_part(3, 0, S, "bank3", nc.vector.tensor_copy)
        first_hop(2, S)
        second_hop(0, S)
        second_hop(1, S)
        first_hop(3, HALF)
        second_hop(2, S)
        second_hop(3, HALF)
